import numpy as np, ml_dtypes
CORES = [1,17,65,89,97,113]
N = 6
F = 256
def setup_inputs(rng):
    return {"ah": rng.standard_normal((N, 128, 128), dtype=np.float32).astype(ml_dtypes.bfloat16), "al": (rng.standard_normal((N, 128, 128), dtype=np.float32) / 256).astype(ml_dtypes.bfloat16), "bh": rng.standard_normal((N, 128, F), dtype=np.float32).astype(ml_dtypes.bfloat16), "bl": (rng.standard_normal((N, 128, F), dtype=np.float32) / 256).astype(ml_dtypes.bfloat16)}
def setup_inputs_big(rng):
    d = setup_inputs(rng)
    for k in ("ah", "al", "bh", "bl"): d[k] = (d[k].astype(np.float32) * 1024.0).astype(d[k].dtype)
    return d
def setup_inputs_small(rng):
    d = setup_inputs(rng)
    for k in ("ah", "al", "bh", "bl"): d[k] = (d[k].astype(np.float32) * (1 / 1024.0)).astype(d[k].dtype)
    return d
def setup_inputs_apart(rng):
    d = setup_inputs(rng)
    f = (10.0 ** rng.permutation(np.linspace(-1.5, 1.5, N))).astype(np.float32).reshape(N, 1, 1)
    for k in ("ah", "al", "bh", "bl"): d[k] = (d[k].astype(np.float32) * f).astype(d[k].dtype)
    return d
def reference(ah, al, bh, bl):
    AH, AL, BH, BL = ah.astype(np.float64), al.astype(np.float64), bh.astype(np.float64), bl.astype(np.float64)
    s = sum((AH[j] + AL[j]).T @ (BH[j] + BL[j]) for j in range(N))
    s = s.astype(np.float32 if ah.dtype != np.float64 else np.float64)
    return {"y": np.broadcast_to(s, (N,) + s.shape)}

@@ -1,0 +1,173 @@
+from concourse.bass import DstId, RemoteDMATransfer
+from concourse.mybir import AluOpType
+
+N = 6
+F = 256
+H = 4
+W = F // H
+NREL = 2
+HALF = F // 2
+
+SCRATCH = {
+    "sah": ("sbuf", [128, 128], "bfloat16"),
+    "sal": ("sbuf", [128, 128], "bfloat16"),
+    "sbh": ("sbuf", [128, F], "bfloat16"),
+    "sbl": ("sbuf", [128, F], "bfloat16"),
+    "ps0": ("psum", [128, 512], "float32"),
+    "ps1": ("psum", [128, 512], "float32"),
+    "p": ("sbuf", [128, F], "float32"),
+    "hop": ("dram", [H, 128, W], "float32"),
+    "slots": ("dram", [N, 128, W], "float32"),
+    "res": ("dram", [H, 128, W], "float32"),
+    "land": ("sbuf", [128, F], "float32"),
+    "out": ("sbuf", [128, F], "float32"),
+}
+SEMAPHORES = ["l_ah", "l_al", "l_bh", "l_bl", "mm0", "mm1", "cp", "sent", "ev", "od", "rin", "es", "ad",
+              "sta", "stb"] + ["r%d" % h for h in range(H)]
+
+
+def _layout(T, topo):
+    cores = list(T.cores)
+    everyone = range(topo.CORES_PER_CHIP * topo.CHIPS)
+
+    def reach(a, b):
+        return a == b or topo.may_write(a, b)
+
+    groups = [[x for x in cores if reach(c, x) and reach(x, c)] for c in cores]
+    main = max(groups, key=len)
+    rest = [c for c in cores if c not in main]
+    assert len(rest) == 1
+
+    def gates(c):
+        return [x for x in everyone if x not in cores and topo.chip(x) == topo.chip(c)
+                and topo.die(x) == topo.die(c) and all(topo.may_write(x, y) for y in cores)]
+
+    hubs = [gates(main[h % len(main)])[h // len(main)] for h in range(H)]
+    relays = [x for x in gates(rest[0]) if all(topo.may_write(x, y) for y in hubs)][:NREL]
+    return main, rest[0], hubs, relays
+
+
+def _dst(topo, c):
+    rid, pid, _ring = topo.addr(c)
+    return DstId(rid=rid, pnc=pid)
+
+
+def _allowed(topo, src, dsts):
+    m = topo.mask(src, dsts[0])
+    for d in dsts[1:]:
+        m &= topo.mask(src, d)
+    return [b for b in range(m.bit_length()) if (m >> b) & 1]
+
+
+def _bits(engines):
+    m = 0
+    for b in engines:
+        m |= 1 << b
+    return m
+
+
+def _partial(g, T):
+    s = T.sem
+    g.sync.dma_start(T.sah[:], T.ah[:]).then_inc(s.l_ah, 16)
+    g.scalar.dma_start(T.sbh[:], T.bh[:]).then_inc(s.l_bh, 16)
+    g.sync.dma_start(T.sbl[:], T.bl[:]).then_inc(s.l_bl, 16)
+    g.scalar.dma_start(T.sal[:], T.al[:]).then_inc(s.l_al, 16)
+    t = g.tensor
+    lo, hi = slice(0, HALF), slice(HALF, F)
+    ps0, ps1 = T.ps0[:, 0:HALF], T.ps1[:, 0:HALF]
+    t.wait_ge(s.l_ah, 16)
+    t.wait_ge(s.l_bh, 16)
+    t.matmul(ps0, T.sah[:], T.sbh[:, lo], True, False).then_inc(s.mm0, 1)
+    t.matmul(ps1, T.sah[:], T.sbh[:, hi], True, False).then_inc(s.mm1, 1)
+    t.wait_ge(s.l_bl, 16)
+    t.matmul(ps0, T.sah[:], T.sbl[:, lo], False, False).then_inc(s.mm0, 1)
+    t.matmul(ps1, T.sah[:], T.sbl[:, hi], False, False).then_inc(s.mm1, 1)
+    t.wait_ge(s.l_al, 16)
+    t.matmul(ps0, T.sal[:], T.sbh[:, lo], False, False).then_inc(s.mm0, 1)
+    t.matmul(ps0, T.sal[:], T.sbl[:, lo], False, True).then_inc(s.mm0, 1)
+    t.matmul(ps1, T.sal[:], T.sbh[:, hi], False, False).then_inc(s.mm1, 1)
+    t.matmul(ps1, T.sal[:], T.sbl[:, hi], False, True).then_inc(s.mm1, 1)
+    v = g.vector
+    v.wait_ge(s.mm0, 4)
+    v.tensor_copy(T.p[:, lo], ps0).then_inc(s.cp, 1)
+    v.wait_ge(s.mm1, 4)
+    v.tensor_copy(T.p[:, hi], ps1).then_inc(s.cp, 1)
+
+
+def rank_program(g, core, T, topo):
+    main, odd, hubs, relays = _layout(T, topo)
+    s = T.sem
+    cores = list(T.cores)
+    cols = [slice(h * W, (h + 1) * W) for h in range(H)]
+    per_main = len(_allowed(topo, main[-1], hubs)) // H
+    per_odd = len(_allowed(topo, odd, relays)) // H
+    mine = {q: [h for h in range(H) if h % len(relays) == k] for k, q in enumerate(relays)}
+
+    if core in main:
+        _partial(g, T)
+        eng = _allowed(topo, core, hubs)
+        g.wait_ge(s.cp, 2)
+        g.remote_dma_fused(
+            [RemoteDMATransfer(dst_ids=[_dst(topo, hubs[h])],
+                               dma_engine_mask=_bits(eng[h * per_main:(h + 1) * per_main]),
+                               remote_sem=s.ev, src=T.p[:, cols[h]], dst=T.slots[cores.index(core)])
+             for h in range(H)], local_sem=s.sent)
+        queues = [(g.sync, s.sta), (g.scalar, s.stb)]
+        count = [0, 0]
+        for h in range(H):
+            k = h * 2 // H
+            q, st = queues[k]
+            q.wait_ge(s["r%d" % h], len(_allowed(topo, hubs[h], main)))
+            q.dma_start(T.y[:, cols[h]], T.res[h]).then_inc(st, 16)
+            count[k] += 16
+        for k in range(2):
+            queues[k][0].wait_ge(queues[k][1], count[k])
+        g.wait_ge(s.sent, per_main * H)
+
+    elif core == odd:
+        _partial(g, T)
+        eng = _allowed(topo, core, relays)
+        g.wait_ge(s.cp, 2)
+        g.remote_dma_fused(
+            [RemoteDMATransfer(dst_ids=[_dst(topo, relays[h % len(relays)])],
+                               dma_engine_mask=_bits(eng[h * per_odd:(h + 1) * per_odd]),
+                               remote_sem=s.rin, src=T.p[:, cols[h]], dst=T.hop[h])
+             for h in range(H)], local_sem=s.sent)
+        v = g.vector
+        v.wait_ge(s.cp, 2)
+        v.wait_ge(s.es, sum(len(_allowed(topo, x, cores)) for x in hubs))
+        v.tensor_tensor(T.out[:], T.land[:], T.p[:], AluOpType.add).then_inc(s.ad, 1)
+        g.sync.wait_ge(s.ad, 1)
+        g.sync.dma_start(T.y[:], T.out[:]).then_inc(s.sta, 16)
+        g.sync.wait_ge(s.sta, 16)
+        g.wait_ge(s.sent, per_odd * H)
+
+    elif core in relays:
+        blocks = mine[core]
+        eng = _allowed(topo, core, hubs)
+        per = len(eng) // len(blocks)
+        g.wait_ge(s.rin, per_odd * len(blocks))
+        g.remote_dma_fused(
+            [RemoteDMATransfer(dst_ids=[_dst(topo, hubs[h])], dma_engine_mask=_bits(eng[k * per:(k + 1) * per]),
+                               remote_sem=s.od, src=T.hop[h], dst=T.slots[cores.index(odd)])
+             for k, h in enumerate(blocks)], local_sem=s.sent)
+        g.wait_ge(s.sent, per * len(blocks))
+
+    elif core in hubs:
+        h = hubs.index(core)
+        eng = _allowed(topo, core, cores)
+        feeder = relays[h % len(relays)]
+        per = len(_allowed(topo, feeder, hubs)) // len(mine[feeder])
+        g.wait_ge(s.ev, per_main * len(main))
+        g.remote_dma_fused(
+            [RemoteDMATransfer(dst_ids=[_dst(topo, odd)], dma_engine_mask=_bits(eng), remote_sem=s.es,
+                               srcs=[T.slots[cores.index(c)] for c in main], dsts=[T.land[:, cols[h]]], alu_op=1)],
+            local_sem=s.sent)
+        g.wait_ge(s.od, per)
+        eng2 = _allowed(topo, core, main)
+        g.remote_dma_fused(
+            [RemoteDMATransfer(dst_ids=[_dst(topo, c) for c in main], dma_engine_mask=_bits(eng2),
+                               remote_sem=s["r%d" % h], srcs=[T.slots[i] for i in range(N)],
+                               dsts=[T.res[h] for _c in main], alu_op=1)],
+            local_sem=s.sent)
+        g.wait_ge(s.sent, len(eng) + len(eng2))

@@ -3,10 +3,11 @@ from concourse.mybir import AluOpType
 
 N = 6
 F = 256
-H = 4
+H = 8
 W = F // H
 NREL = 2
 HALF = F // 2
+NEAR = 4
 
 SCRATCH = {
     "sah": ("sbuf", [128, 128], "bfloat16"),
@@ -22,8 +23,8 @@ SCRATCH = {
     "land": ("sbuf", [128, F], "float32"),
     "out": ("sbuf", [128, F], "float32"),
 }
-SEMAPHORES = ["l_ah", "l_al", "l_bh", "l_bl", "mm0", "mm1", "cp", "sent", "ev", "od", "rin", "es", "ad",
-              "sta", "stb"] + ["r%d" % h for h in range(H)]
+SEMAPHORES = ["l_ah", "l_al", "l_bh", "l_bl", "mm0", "mm1", "cp0", "cp1", "sent", "ev", "od", "rin0", "rin1", "es",
+              "ad", "sta", "stb"] + ["r%d" % h for h in range(H)]
 
 
 def _layout(T, topo):
@@ -81,93 +82,115 @@ def _partial(g, T):
     t.matmul(ps1, T.sah[:], T.sbh[:, hi], True, False).then_inc(s.mm1, 1)
     t.wait_ge(s.l_bl, 16)
     t.matmul(ps0, T.sah[:], T.sbl[:, lo], False, False).then_inc(s.mm0, 1)
-    t.matmul(ps1, T.sah[:], T.sbl[:, hi], False, False).then_inc(s.mm1, 1)
     t.wait_ge(s.l_al, 16)
     t.matmul(ps0, T.sal[:], T.sbh[:, lo], False, False).then_inc(s.mm0, 1)
     t.matmul(ps0, T.sal[:], T.sbl[:, lo], False, True).then_inc(s.mm0, 1)
+    t.matmul(ps1, T.sah[:], T.sbl[:, hi], False, False).then_inc(s.mm1, 1)
     t.matmul(ps1, T.sal[:], T.sbh[:, hi], False, False).then_inc(s.mm1, 1)
     t.matmul(ps1, T.sal[:], T.sbl[:, hi], False, True).then_inc(s.mm1, 1)
     v = g.vector
     v.wait_ge(s.mm0, 4)
-    v.tensor_copy(T.p[:, lo], ps0).then_inc(s.cp, 1)
+    v.tensor_copy(T.p[:, lo], ps0).then_inc(s.cp0, 1)
     v.wait_ge(s.mm1, 4)
-    v.tensor_copy(T.p[:, hi], ps1).then_inc(s.cp, 1)
+    v.tensor_copy(T.p[:, hi], ps1).then_inc(s.cp1, 1)
 
 
 def rank_program(g, core, T, topo):
     main, odd, hubs, relays = _layout(T, topo)
     s = T.sem
     cores = list(T.cores)
+    nm = len(main)
+    nrel = len(relays)
     cols = [slice(h * W, (h + 1) * W) for h in range(H)]
-    per_main = len(_allowed(topo, main[-1], hubs)) // H
-    per_odd = len(_allowed(topo, odd, relays)) // H
-    mine = {q: [h for h in range(H) if h % len(relays) == k] for k, q in enumerate(relays)}
+    waves = [[h for h in range(H) if (h * W < HALF) == (w == 0)] for w in range(2)]
+    nw = len(waves[0])
+    per_main = len(_allowed(topo, main[-1], hubs)) // nw
+    per_odd = len(_allowed(topo, odd, relays)) // nw
+    per_relay = len(_allowed(topo, relays[0], hubs)) // (nw // nrel)
+
+    def far(x):
+        return _allowed(topo, x, main)
+
+    def near(x):
+        home = [c for c in main if topo.chip(c) == topo.chip(x)]
+        return [b for b in _allowed(topo, x, home) if b not in far(x)][:NEAR]
 
     if core in main:
         _partial(g, T)
         eng = _allowed(topo, core, hubs)
-        g.wait_ge(s.cp, 2)
-        g.remote_dma_fused(
-            [RemoteDMATransfer(dst_ids=[_dst(topo, hubs[h])],
-                               dma_engine_mask=_bits(eng[h * per_main:(h + 1) * per_main]),
-                               remote_sem=s.ev, src=T.p[:, cols[h]], dst=T.slots[cores.index(core)])
-             for h in range(H)], local_sem=s.sent)
+        for w in range(2):
+            g.wait_ge(s["cp%d" % w], 1)
+            g.remote_dma_fused(
+                [RemoteDMATransfer(dst_ids=[_dst(topo, hubs[h])],
+                                   dma_engine_mask=_bits(eng[k * per_main:(k + 1) * per_main]),
+                                   remote_sem=s.ev, src=T.p[:, cols[h]], dst=T.slots[cores.index(core)])
+                 for k, h in enumerate(waves[w])], local_sem=s.sent)
         queues = [(g.sync, s.sta), (g.scalar, s.stb)]
         count = [0, 0]
-        for h in range(H):
-            k = h * 2 // H
-            q, st = queues[k]
-            q.wait_ge(s["r%d" % h], len(_allowed(topo, hubs[h], main)))
+
+        def home(h):
+            return topo.chip(hubs[h]) == topo.chip(core)
+
+        def when(h):
+            return (h * W >= HALF, nm // 2 if home(h) else (main.index(core) - h) % nm)
+
+        for k, h in enumerate(sorted(range(H), key=when)):
+            q, st = queues[k % 2]
+            q.wait_ge(s["r%d" % h], len(near(hubs[h]) if home(h) else far(hubs[h])))
             q.dma_start(T.y[:, cols[h]], T.res[h]).then_inc(st, 16)
-            count[k] += 16
+            count[k % 2] += 16
         for k in range(2):
             queues[k][0].wait_ge(queues[k][1], count[k])
-        g.wait_ge(s.sent, per_main * H)
+        g.wait_ge(s.sent, 2 * per_main * nw)
 
     elif core == odd:
         _partial(g, T)
         eng = _allowed(topo, core, relays)
-        g.wait_ge(s.cp, 2)
-        g.remote_dma_fused(
-            [RemoteDMATransfer(dst_ids=[_dst(topo, relays[h % len(relays)])],
-                               dma_engine_mask=_bits(eng[h * per_odd:(h + 1) * per_odd]),
-                               remote_sem=s.rin, src=T.p[:, cols[h]], dst=T.hop[h])
-             for h in range(H)], local_sem=s.sent)
+        for w in range(2):
+            g.wait_ge(s["cp%d" % w], 1)
+            g.remote_dma_fused(
+                [RemoteDMATransfer(dst_ids=[_dst(topo, relays[k % nrel])],
+                                   dma_engine_mask=_bits(eng[k * per_odd:(k + 1) * per_odd]),
+                                   remote_sem=s["rin%d" % w], src=T.p[:, cols[h]], dst=T.hop[h])
+                 for k, h in enumerate(waves[w])], local_sem=s.sent)
         v = g.vector
-        v.wait_ge(s.cp, 2)
+        v.wait_ge(s.cp0, 1)
+        v.wait_ge(s.cp1, 1)
         v.wait_ge(s.es, sum(len(_allowed(topo, x, cores)) for x in hubs))
         v.tensor_tensor(T.out[:], T.land[:], T.p[:], AluOpType.add).then_inc(s.ad, 1)
         g.sync.wait_ge(s.ad, 1)
         g.sync.dma_start(T.y[:], T.out[:]).then_inc(s.sta, 16)
         g.sync.wait_ge(s.sta, 16)
-        g.wait_ge(s.sent, per_odd * H)
+        g.wait_ge(s.sent, 2 * per_odd * nw)
 
     elif core in relays:
-        blocks = mine[core]
         eng = _allowed(topo, core, hubs)
-        per = len(eng) // len(blocks)
-        g.wait_ge(s.rin, per_odd * len(blocks))
-        g.remote_dma_fused(
-            [RemoteDMATransfer(dst_ids=[_dst(topo, hubs[h])], dma_engine_mask=_bits(eng[k * per:(k + 1) * per]),
-                               remote_sem=s.od, src=T.hop[h], dst=T.slots[cores.index(odd)])
-             for k, h in enumerate(blocks)], local_sem=s.sent)
-        g.wait_ge(s.sent, per * len(blocks))
+        for w in range(2):
+            blocks = [h for k, h in enumerate(waves[w]) if relays[k % nrel] == core]
+            g.wait_ge(s["rin%d" % w], per_odd * len(blocks))
+            g.remote_dma_fused(
+                [RemoteDMATransfer(dst_ids=[_dst(topo, hubs[h])],
+                                   dma_engine_mask=_bits(eng[k * per_relay:(k + 1) * per_relay]),
+                                   remote_sem=s.od, src=T.hop[h], dst=T.slots[cores.index(odd)])
+                 for k, h in enumerate(blocks)], local_sem=s.sent)
+        g.wait_ge(s.sent, 2 * per_relay * (nw // nrel))
 
     elif core in hubs:
         h = hubs.index(core)
         eng = _allowed(topo, core, cores)
-        feeder = relays[h % len(relays)]
-        per = len(_allowed(topo, feeder, hubs)) // len(mine[feeder])
-        g.wait_ge(s.ev, per_main * len(main))
+        g.wait_ge(s.ev, per_main * nm)
         g.remote_dma_fused(
             [RemoteDMATransfer(dst_ids=[_dst(topo, odd)], dma_engine_mask=_bits(eng), remote_sem=s.es,
                                srcs=[T.slots[cores.index(c)] for c in main], dsts=[T.land[:, cols[h]]], alu_op=1)],
             local_sem=s.sent)
-        g.wait_ge(s.od, per)
-        eng2 = _allowed(topo, core, main)
-        g.remote_dma_fused(
-            [RemoteDMATransfer(dst_ids=[_dst(topo, c) for c in main], dma_engine_mask=_bits(eng2),
-                               remote_sem=s["r%d" % h], srcs=[T.slots[i] for i in range(N)],
-                               dsts=[T.res[h] for _c in main], alu_op=1)],
-            local_sem=s.sent)
-        g.wait_ge(s.sent, len(eng) + len(eng2))
+        g.wait_ge(s.od, per_relay)
+        served = main[h % nm:] + main[:h % nm]
+        left = len(eng)
+        for who, engines in [(served[1:], far(core)), (served[:1], near(core))]:
+            g.remote_dma_fused(
+                [RemoteDMATransfer(dst_ids=[_dst(topo, c) for c in who], dma_engine_mask=_bits(engines),
+                                   remote_sem=s["r%d" % h], srcs=[T.slots[i] for i in range(N)],
+                                   dsts=[T.res[h] for _c in who], alu_op=1)],
+                local_sem=s.sent)
+            left += len(engines)
+        g.wait_ge(s.sent, left)

from concourse.bass import DstId, RemoteDMATransfer
from concourse.mybir import AluOpType

N = 6
F = 256
H = 8
W = F // H
NREL = 2
HALF = F // 2
NEAR = 4

SCRATCH = {
    "sah": ("sbuf", [128, 128], "bfloat16"),
    "sal": ("sbuf", [128, 128], "bfloat16"),
    "sbh": ("sbuf", [128, F], "bfloat16"),
    "sbl": ("sbuf", [128, F], "bfloat16"),
    "ps0": ("psum", [128, 512], "float32"),
    "ps1": ("psum", [128, 512], "float32"),
    "p": ("sbuf", [128, F], "float32"),
    "hop": ("dram", [H, 128, W], "float32"),
    "slots": ("dram", [N, 128, W], "float32"),
    "res": ("dram", [H, 128, W], "float32"),
    "land": ("sbuf", [128, F], "float32"),
    "out": ("sbuf", [128, F], "float32"),
}
SEMAPHORES = ["l_ah", "l_al", "l_bh", "l_bl", "mm0", "mm1", "cp0", "cp1", "sent", "ev", "od", "rin0", "rin1", "es",
              "ad", "sta", "stb"] + ["r%d" % h for h in range(H)]


def _layout(T, topo):
    cores = list(T.cores)
    everyone = range(topo.CORES_PER_CHIP * topo.CHIPS)

    def reach(a, b):
        return a == b or topo.may_write(a, b)

    groups = [[x for x in cores if reach(c, x) and reach(x, c)] for c in cores]
    main = max(groups, key=len)
    rest = [c for c in cores if c not in main]
    assert len(rest) == 1

    def gates(c):
        return [x for x in everyone if x not in cores and topo.chip(x) == topo.chip(c)
                and topo.die(x) == topo.die(c) and all(topo.may_write(x, y) for y in cores)]

    hubs = [gates(main[h % len(main)])[h // len(main)] for h in range(H)]
    relays = [x for x in gates(rest[0]) if all(topo.may_write(x, y) for y in hubs)][:NREL]
    return main, rest[0], hubs, relays


def _dst(topo, c):
    rid, pid, _ring = topo.addr(c)
    return DstId(rid=rid, pnc=pid)


def _allowed(topo, src, dsts):
    m = topo.mask(src, dsts[0])
    for d in dsts[1:]:
        m &= topo.mask(src, d)
    return [b for b in range(m.bit_length()) if (m >> b) & 1]


def _bits(engines):
    m = 0
    for b in engines:
        m |= 1 << b
    return m


def _partial(g, T):
    s = T.sem
    g.sync.dma_start(T.sah[:], T.ah[:]).then_inc(s.l_ah, 16)
    g.scalar.dma_start(T.sbh[:], T.bh[:]).then_inc(s.l_bh, 16)
    g.sync.dma_start(T.sbl[:], T.bl[:]).then_inc(s.l_bl, 16)
    g.scalar.dma_start(T.sal[:], T.al[:]).then_inc(s.l_al, 16)
    t = g.tensor
    lo, hi = slice(0, HALF), slice(HALF, F)
    ps0, ps1 = T.ps0[:, 0:HALF], T.ps1[:, 0:HALF]
    t.wait_ge(s.l_ah, 16)
    t.wait_ge(s.l_bh, 16)
    t.matmul(ps0, T.sah[:], T.sbh[:, lo], True, False).then_inc(s.mm0, 1)
    t.matmul(ps1, T.sah[:], T.sbh[:, hi], True, False).then_inc(s.mm1, 1)
    t.wait_ge(s.l_bl, 16)
    t.matmul(ps0, T.sah[:], T.sbl[:, lo], False, False).then_inc(s.mm0, 1)
    t.wait_ge(s.l_al, 16)
    t.matmul(ps0, T.sal[:], T.sbh[:, lo], False, False).then_inc(s.mm0, 1)
    t.matmul(ps0, T.sal[:], T.sbl[:, lo], False, True).then_inc(s.mm0, 1)
    t.matmul(ps1, T.sah[:], T.sbl[:, hi], False, False).then_inc(s.mm1, 1)
    t.matmul(ps1, T.sal[:], T.sbh[:, hi], False, False).then_inc(s.mm1, 1)
    t.matmul(ps1, T.sal[:], T.sbl[:, hi], False, True).then_inc(s.mm1, 1)
    v = g.vector
    v.wait_ge(s.mm0, 4)
    v.tensor_copy(T.p[:, lo], ps0).then_inc(s.cp0, 1)
    v.wait_ge(s.mm1, 4)
    v.tensor_copy(T.p[:, hi], ps1).then_inc(s.cp1, 1)


def rank_program(g, core, T, topo):
    main, odd, hubs, relays = _layout(T, topo)
    s = T.sem
    cores = list(T.cores)
    nm = len(main)
    nrel = len(relays)
    cols = [slice(h * W, (h + 1) * W) for h in range(H)]
    waves = [[h for h in range(H) if (h * W < HALF) == (w == 0)] for w in range(2)]
    nw = len(waves[0])
    per_main = len(_allowed(topo, main[-1], hubs)) // nw
    per_odd = len(_allowed(topo, odd, relays)) // nw
    per_relay = len(_allowed(topo, relays[0], hubs)) // (nw // nrel)

    def far(x):
        return _allowed(topo, x, main)

    def near(x):
        home = [c for c in main if topo.chip(c) == topo.chip(x)]
        return [b for b in _allowed(topo, x, home) if b not in far(x)][:NEAR]

    if core in main:
        _partial(g, T)
        eng = _allowed(topo, core, hubs)
        for w in range(2):
            g.wait_ge(s["cp%d" % w], 1)
            g.remote_dma_fused(
                [RemoteDMATransfer(dst_ids=[_dst(topo, hubs[h])],
                                   dma_engine_mask=_bits(eng[k * per_main:(k + 1) * per_main]),
                                   remote_sem=s.ev, src=T.p[:, cols[h]], dst=T.slots[cores.index(core)])
                 for k, h in enumerate(waves[w])], local_sem=s.sent)
        queues = [(g.sync, s.sta), (g.scalar, s.stb)]
        count = [0, 0]

        def home(h):
            return topo.chip(hubs[h]) == topo.chip(core)

        def when(h):
            return (h * W >= HALF, nm // 2 if home(h) else (main.index(core) - h) % nm)

        for k, h in enumerate(sorted(range(H), key=when)):
            q, st = queues[k % 2]
            q.wait_ge(s["r%d" % h], len(near(hubs[h]) if home(h) else far(hubs[h])))
            q.dma_start(T.y[:, cols[h]], T.res[h]).then_inc(st, 16)
            count[k % 2] += 16
        for k in range(2):
            queues[k][0].wait_ge(queues[k][1], count[k])
        g.wait_ge(s.sent, 2 * per_main * nw)

    elif core == odd:
        _partial(g, T)
        eng = _allowed(topo, core, relays)
        for w in range(2):
            g.wait_ge(s["cp%d" % w], 1)
            g.remote_dma_fused(
                [RemoteDMATransfer(dst_ids=[_dst(topo, relays[k % nrel])],
                                   dma_engine_mask=_bits(eng[k * per_odd:(k + 1) * per_odd]),
                                   remote_sem=s["rin%d" % w], src=T.p[:, cols[h]], dst=T.hop[h])
                 for k, h in enumerate(waves[w])], local_sem=s.sent)
        v = g.vector
        v.wait_ge(s.cp0, 1)
        v.wait_ge(s.cp1, 1)
        v.wait_ge(s.es, sum(len(_allowed(topo, x, cores)) for x in hubs))
        v.tensor_tensor(T.out[:], T.land[:], T.p[:], AluOpType.add).then_inc(s.ad, 1)
        g.sync.wait_ge(s.ad, 1)
        g.sync.dma_start(T.y[:], T.out[:]).then_inc(s.sta, 16)
        g.sync.wait_ge(s.sta, 16)
        g.wait_ge(s.sent, 2 * per_odd * nw)

    elif core in relays:
        eng = _allowed(topo, core, hubs)
        for w in range(2):
            blocks = [h for k, h in enumerate(waves[w]) if relays[k % nrel] == core]
            g.wait_ge(s["rin%d" % w], per_odd * len(blocks))
            g.remote_dma_fused(
                [RemoteDMATransfer(dst_ids=[_dst(topo, hubs[h])],
                                   dma_engine_mask=_bits(eng[k * per_relay:(k + 1) * per_relay]),
                                   remote_sem=s.od, src=T.hop[h], dst=T.slots[cores.index(odd)])
                 for k, h in enumerate(blocks)], local_sem=s.sent)
        g.wait_ge(s.sent, 2 * per_relay * (nw // nrel))

    elif core in hubs:
        h = hubs.index(core)
        eng = _allowed(topo, core, cores)
        g.wait_ge(s.ev, per_main * nm)
        g.remote_dma_fused(
            [RemoteDMATransfer(dst_ids=[_dst(topo, odd)], dma_engine_mask=_bits(eng), remote_sem=s.es,
                               srcs=[T.slots[cores.index(c)] for c in main], dsts=[T.land[:, cols[h]]], alu_op=1)],
            local_sem=s.sent)
        g.wait_ge(s.od, per_relay)
        served = main[h % nm:] + main[:h % nm]
        left = len(eng)
        for who, engines in [(served[1:], far(core)), (served[:1], near(core))]:
            g.remote_dma_fused(
                [RemoteDMATransfer(dst_ids=[_dst(topo, c) for c in who], dma_engine_mask=_bits(engines),
                                   remote_sem=s["r%d" % h], srcs=[T.slots[i] for i in range(N)],
                                   dsts=[T.res[h] for _c in who], alu_op=1)],
                local_sem=s.sent)
            left += len(engines)
        g.wait_ge(s.sent, left)
